import numpy as np
import ml_dtypes


def mxq(x, axis, fmt="e4m3"):
    dtype, down = {"e4m3": (ml_dtypes.float8_e4m3fn, 7), "e5m2": (ml_dtypes.float8_e5m2, 14)}[fmt]
    v = np.moveaxis(np.asarray(x, np.float32).astype(ml_dtypes.bfloat16).astype(np.float64), axis, -1)
    blocks = v.reshape(v.shape[:-1] + (-1, 32))
    amax = np.abs(blocks).max(-1, keepdims=True)
    byte = np.maximum(np.where(amax > 0, np.frexp(amax)[1] - 1 + 127, 0) - down, 1)
    scale = np.exp2(byte - 127.0)
    codes = (blocks / scale).astype(np.float32).astype(dtype).astype(np.float64)
    return np.moveaxis((codes * scale).reshape(v.shape), -1, axis)


WIDE = False


def mx_kscale(k):
    if not WIDE:
        return np.ones(k)
    levels = np.array([10, -10, 5, -5, 0])
    if k % 512:
        return np.exp2(np.random.permutation(np.resize(levels, k // 32))).repeat(32)
    a = np.empty((k // 512, 16))
    for p in range(k // 512):
        a[p, :8] = np.random.permutation(np.resize(levels, 8))
        for g in range(8):
            far = levels[np.abs(levels - a[p, g]) >= 10]
            a[p, g + 8] = far[np.random.randint(len(far))]
    return np.exp2(a.ravel()).repeat(32)


def f64(x):
    return np.asarray(x).astype(np.float64)


def striped(idx):
    return np.tile(idx.reshape(-1, 16).T, (8, 1)).astype(np.uint16)


def unstriped(offs):
    return offs[:16].T.reshape(-1).astype(np.int64)


E2M1 = np.array([0.0, 0.5, 1.0, 1.5, 2.0, 3.0, 4.0, 6.0, -0.0, -0.5, -1.0, -1.5, -2.0, -3.0, -4.0, -6.0])


def pack_weight(w, fmt):
    k, n = w.shape
    w = f64(np.asarray(w, np.float32).astype(ml_dtypes.bfloat16)).reshape(k // 32, 32, n)
    amax = np.abs(w).max(1)
    if fmt == "e4m3":
        byte = np.frexp(amax)[1] - 1 + 127 - 7
    else:
        mant, ex = np.frexp(amax / 6.0)
        byte = np.where(mant > 0.5, ex, ex - 1) + 127
    byte = np.clip(np.where(amax > 0, byte, 1), 1, 254)
    scaled = (w * np.exp2(127.0 - byte)[:, None, :]).reshape(k, n).astype(np.float32)
    by_word = np.ascontiguousarray(scaled.reshape(k // 512, 128, 4, n).transpose(0, 1, 3, 2))
    if fmt == "e4m3":
        words = by_word.astype(ml_dtypes.float8_e4m3fn).view(np.uint8)
    else:
        c = by_word.astype(ml_dtypes.float4_e2m1fn).view(np.uint8) & 0xF
        words = (c[..., 0::2] | (c[..., 1::2] << 4)).reshape(k // 512, 128, 2 * n)
    return np.ascontiguousarray(words), np.ascontiguousarray(byte.astype(np.uint8).reshape(k // 512, 16, n))


def unpack_weight(words, scales, fmt):
    g, _, n = scales.shape
    words = np.ascontiguousarray(words).reshape(g, 128, n, -1)
    if fmt == "e4m3":
        vals = words.view(ml_dtypes.float8_e4m3fn).astype(np.float64)
    else:
        nib = np.empty((g, 128, n, 4), np.uint8)
        nib[..., 0::2] = words & 0xF
        nib[..., 1::2] = words >> 4
        vals = E2M1[nib]
    vals = vals * np.repeat(np.exp2(scales.astype(np.float64) - 127.0), 8, axis=1)[..., None]
    return vals.transpose(0, 1, 3, 2).reshape(g * 512, n)


def gelu(v):
    return 0.5 * v * (1.0 + np.tanh(np.sqrt(2.0 / np.pi) * (v + 0.044715 * v**3)))


K, H, N, T, S, P = 512, 1024, 384, 2048, 1024, 512

def setup_inputs():
    n = np.random.standard_normal
    s = mx_kscale(K)[:, None]
    u = mx_kscale(H)[:, None]
    d = {}
    d["tab_words"], d["tab_scales"] = pack_weight(n((K, T)) * s, "e2m1")
    d["offs"] = striped(np.random.permutation(T)[:S])
    d["pos1"] = striped(np.random.permutation(S)[:P])
    d["pos2"] = striped(np.random.permutation(S)[:P])
    d["w1"] = (1.5 * n((K, H)) / K ** 0.5 / s).astype(np.float32)
    d["gt"] = (np.exp(0.3 * n(H)) * u[:, 0]).astype(np.float32)
    d["w2_words"], d["w2_scales"] = pack_weight(1.9 * n((H, H)) / H ** 0.5 / u, "e4m3")
    d["gz"] = (np.exp(0.3 * n(H)) * u[:, 0]).astype(np.float32)
    d["w3_words"], d["w3_scales"] = pack_weight(1.1 * n((H, N)) / H ** 0.5 / u, "e2m1")
    return d

def reference(tab_words, tab_scales, offs, pos1, pos2, w1, gt, w2_words, w2_scales, gz, w3_words, w3_scales):
    v = unpack_weight(tab_words, tab_scales, "e2m1")[:, unstriped(offs)]
    w2 = unpack_weight(w2_words, w2_scales, "e4m3")
    w3 = unpack_weight(w3_words, w3_scales, "e2m1")
    a = mxq(f64(w1), 0, "e4m3").T @ v
    x = np.tanh(a) * f64(gt)[:, None]
    b = w2.T @ mxq(x, 0, "e4m3")
    top = np.maximum(a, b)
    z = (top[:, unstriped(pos1)] - top[:, unstriped(pos2)]) * f64(gz)[:, None]
    y = w3.T @ mxq(z, 0, "e4m3")
    return 1.0 / (1.0 + np.exp(-y))

@@ -1,0 +1,269 @@
+from contextlib import ExitStack
+
+import concourse.mybir as mybir
+
+K, H, N, T, S, PAIRS = 512, 1024, 384, 2048, 1024, 512
+FLOPS = 2 * K * H * S + 2 * H * H * S + 2 * H * N * PAIRS
+
+F32 = mybir.dt.float32
+BF16 = mybir.dt.bfloat16
+I32 = mybir.dt.int32
+U32 = mybir.dt.uint32
+U16 = mybir.dt.uint16
+U8 = mybir.dt.uint8
+FP8X4 = mybir.dt.float8_e4m3fn_x4
+FP4X4 = mybir.dt.float4_e2m1fn_x4
+ALU = mybir.AluOpType
+ACT = mybir.ActivationFunctionType
+
+P = 128
+PACK = 4
+PASS = P * PACK
+HALF = 512
+CHUNK = 128
+
+
+def tile_list_cuckoo_host_rejection_kernel(
+    tc, tab_words, tab_scales, offs, pos1, pos2, w1, gt, w2_words, w2_scales, gz, w3_words, w3_scales, out
+):
+    nc = tc.nc
+    with ExitStack() as ctx:
+        keep = ctx.enter_context(tc.tile_pool(name="keep", bufs=1))
+        ring = ctx.enter_context(tc.tile_pool(name="ring", bufs=3))
+        psum = ctx.enter_context(tc.psum_pool(name="psum", bufs=4))
+
+        offs_sb = keep.tile([P, S // 16], U16, name="offs_sb")
+        pos1_sb = keep.tile([P, PAIRS // 16], U16, name="pos1_sb")
+        pos2_sb = keep.tile([P, PAIRS // 16], U16, name="pos2_sb")
+        tabw = keep.tile([P, T], U16, name="tabw", align_bytes=64)
+        tabs = keep.tile([P, T], U8, name="tabs", align_bytes=64)
+        w2s_raw = keep.tile([P, H], U8, name="w2s_raw", align_bytes=64)
+        w3s = keep.tile([P, 2, N], U8, name="w3s", align_bytes=64)
+        w3w = keep.tile([P, 2, 2 * N], U8, name="w3w", align_bytes=64)
+        gt_sb = keep.tile([P, 2, PACK], F32, name="gt_sb")
+        gz_sb = keep.tile([P, 2, PACK], F32, name="gz_sb")
+        warm = keep.tile([P, 8], F32, name="warm")
+        warm2 = keep.tile([P, 8], F32, name="warm2")
+
+        nc.vector.memset(tabs[:].bitcast(I32), 0)
+        nc.vector.memset(warm[:], 0.0)
+        nc.vector.memset(w2s_raw[:].bitcast(I32), 0)
+        nc.vector.memset(w3s[:].rearrange("p a n -> p (a n)").bitcast(I32), 0)
+        nc.scalar.activation(warm2[:], warm[:], ACT.Tanh)
+
+        nc.sync.dma_start(offs_sb[:], offs)
+        nc.sync.dma_start(tabw[:].bitcast(I32), tab_words[0].bitcast(I32))
+        for q in range(4):
+            nc.scalar.dma_start(tabs[32 * q : 32 * q + 4, :].bitcast(I32), tab_scales[0, 4 * q : 4 * q + 4, :].bitcast(I32))
+        w1_raw = []
+        for piece in range(4):
+            raw = keep.tile([P, PACK, 256], F32, name="w1_raw%d" % piece)
+            nc.sync.dma_start(raw[:], w1[:, 256 * piece : 256 * (piece + 1)].rearrange("(p j) c -> p j c", j=PACK))
+            w1_raw.append(raw)
+            if piece == 1:
+                nc.sync.dma_start(gt_sb[:], gt.rearrange("(b p t) -> p b t", p=P, t=PACK))
+        w2_raw = []
+        for g in range(2):
+            raw = keep.tile([P, H], U32, name="w2_raw%d" % g)
+            nc.sync.dma_start(raw[:].bitcast(I32), w2_words[g].rearrange("p c i -> p (c i)").bitcast(I32))
+            w2_raw.append(raw)
+        for q in range(4):
+            nc.sync.dma_start(w2s_raw[32 * q : 32 * q + 8, :].bitcast(I32), w2_scales[:, 4 * q : 4 * q + 4, :].bitcast(I32))
+        nc.sync.dma_start(pos2_sb[:], pos2)
+        nc.sync.dma_start(pos1_sb[:], pos1)
+        nc.sync.dma_start(gz_sb[:], gz.rearrange("(b p t) -> p b t", p=P, t=PACK))
+        nc.sync.dma_start(w3w[:].bitcast(I32), w3_words.rearrange("a p c -> p a c").bitcast(I32))
+        for q in range(4):
+            nc.sync.dma_start(
+                w3s[32 * q : 32 * q + 4, :, :].bitcast(I32),
+                w3_scales[:, 4 * q : 4 * q + 4, :].rearrange("a r n -> r a n").bitcast(I32),
+            )
+
+        vw = [keep.tile([P, HALF], U16, name="vw%d" % h, align_bytes=64) for h in range(2)]
+        vs = [keep.tile([P, HALF], U8, name="vs%d" % h, align_bytes=64) for h in range(2)]
+
+        def gather_table(h):
+            part = offs_sb[:, 32 * h : 32 * (h + 1)]
+            nc.vector.tensor_copy(vw[h][:], tabw[:].indirect(part))
+            nc.vector.tensor_copy(vs[h][:], tabs[:].indirect(part))
+
+        w1g = [keep.tile([P, PASS * PACK], BF16, name="w1g%d" % b, align_bytes=64) for b in range(2)]
+        w1c = [keep.tile([P, PASS], U32, name="w1c%d" % b, align_bytes=64) for b in range(2)]
+        w1s = [keep.tile([P, PASS], U8, name="w1s%d" % b, align_bytes=64) for b in range(2)]
+
+        def cast_w1(piece):
+            b, part = divmod(piece, 2)
+            dst = w1g[b][:].rearrange("p (t q j) -> p q t j", t=PACK, j=PACK)[:, 64 * part : 64 * (part + 1), :, :]
+            nc.scalar.copy(dst, w1_raw[piece][:].rearrange("p j (q t) -> p q t j", t=PACK))
+
+        def quantize_w1(b):
+            nc.vector.quantize_mx(w1c[b][:].bitcast(FP8X4), w1s[b][:], w1g[b][:])
+
+        w2c = [keep.tile([P, H], U32, name="w2c%d" % g, align_bytes=64) for g in range(2)]
+        w2s = keep.tile([P, H], U8, name="w2s", align_bytes=64)
+
+        def deal_w2_words(g):
+            nc.vector.tensor_copy(
+                w2c[g][:].rearrange("p (b t u i) -> p b u t i", b=2, t=PACK, i=4),
+                w2_raw[g][:].rearrange("p (b u i t) -> p b u t i", b=2, t=PACK, i=4),
+            )
+
+        def deal_w2_scales():
+            nc.vector.tensor_copy(
+                w2s[:].rearrange("p (b t u i) -> p b u t i", b=2, t=PACK, i=16),
+                w2s_raw[:].rearrange("p (b u i t) -> p b u t i", b=2, t=PACK, i=16),
+            )
+
+        a_sb = {(b, h): keep.tile([P, PACK, HALF], F32, name="a_sb%d%d" % (b, h)) for b in range(2) for h in range(2)}
+        xc = {(b, h): keep.tile([P, HALF], U32, name="xc%d%d" % (b, h), align_bytes=64) for b in range(2) for h in range(2)}
+        xs = {(b, h): keep.tile([P, HALF], U8, name="xs%d%d" % (b, h), align_bytes=64) for b in range(2) for h in range(2)}
+        top = [keep.tile([P, S], F32, name="top%d" % m) for m in range(8)]
+        banks, tanh_tiles, x_tiles = {}, {}, {}
+
+        def first_product(b, h, c):
+            bank = psum.tile([P, PACK, CHUNK], F32, name="bank_a", tag="a")
+            cols = slice(CHUNK * c, CHUNK * (c + 1))
+            for t in range(PACK):
+                rows = slice(P * t, P * (t + 1))
+                nc.tensor.matmul_mx(
+                    bank[:, t, :], lhsT=w1c[b][:, rows].bitcast(FP8X4), lhsT_scale=w1s[b][:, rows],
+                    rhs=vw[h][:, cols].bitcast(FP4X4), rhs_scale=vs[h][:, cols], start=True, stop=True,
+                )
+            banks[b, h, c] = bank
+
+        def tanh_of(b, h, c):
+            if c % 2 == 0:
+                tanh_tiles[b, h, c // 2] = ring.tile([P, 2 * CHUNK, PACK], F32, name="th", tag="th")
+            dst = tanh_tiles[b, h, c // 2][:, CHUNK * (c % 2) : CHUNK * (c % 2 + 1), :]
+            nc.scalar.activation(dst, banks[b, h, c][:].rearrange("p t n -> p n t"), ACT.Tanh)
+
+        def keep_a(b, h, c):
+            nc.scalar.copy(a_sb[b, h][:, :, CHUNK * c : CHUNK * (c + 1)], banks[b, h, c][:])
+
+        def gate_x(b, h, u):
+            xg = ring.tile([P, 2 * CHUNK, PACK], BF16, name="xg", tag="xg", align_bytes=64)
+            gain = gt_sb[:, b, :].unsqueeze(1).to_broadcast([P, 2 * CHUNK, PACK])
+            nc.vector.tensor_tensor(xg[:], tanh_tiles[b, h, u][:], gain, ALU.mult)
+            x_tiles[b, h, u] = xg
+
+        def quantize_x(b, h, u):
+            cols = slice(2 * CHUNK * u, 2 * CHUNK * (u + 1))
+            nc.vector.quantize_mx(
+                xc[b, h][:, cols].bitcast(FP8X4), xs[b, h][:, cols], x_tiles[b, h, u][:].rearrange("p n t -> p (n t)")
+            )
+
+        def second_product(m, h):
+            bank = psum.tile([P, HALF], F32, name="bank_b", tag="b")
+            rows = slice(P * m, P * (m + 1))
+            for g in range(2):
+                nc.tensor.matmul_mx(
+                    bank[:], lhsT=w2c[g][:, rows].bitcast(FP8X4), lhsT_scale=w2s[4 * g : P, rows],
+                    rhs=xc[g, h][:].bitcast(FP8X4), rhs_scale=xs[g, h][:], start=(g == 0), stop=(g == 1),
+                )
+            b, t = divmod(m, PACK)
+            nc.vector.tensor_tensor(top[m][:, HALF * h : HALF * (h + 1)], bank[:], a_sb[b, h][:, t, :], ALU.max)
+
+        gather_table(0)
+        cast_w1(0)
+        cast_w1(1)
+        quantize_w1(0)
+        gather_table(1)
+        steps = [(b, h, u) for h in range(2) for b in range(2) for u in range(2)]
+        for i, (b, h, u) in enumerate(steps):
+            for c in (2 * u, 2 * u + 1):
+                first_product(b, h, c)
+                tanh_of(b, h, c)
+            if i == 0:
+                cast_w1(2)
+                cast_w1(3)
+                quantize_w1(1)
+            gate_x(b, h, u)
+            if i < 6:
+                keep_a(b, h, 2 * u)
+                keep_a(b, h, 2 * u + 1)
+            if i > 0:
+                quantize_x(*steps[i - 1])
+            if i == 1:
+                deal_w2_words(0)
+                deal_w2_scales()
+            if i == 2:
+                deal_w2_words(1)
+            if i >= 4:
+                second_product(2 * (i - 4), 0)
+                second_product(2 * (i - 4) + 1, 0)
+        quantize_x(*steps[-1])
+        for c in range(4):
+            keep_a(1, 1, c)
+
+        WIDTH = 256
+        zc = {(b, u): keep.tile([P, WIDTH], U32, name="zc%d%d" % (b, u), align_bytes=64) for b in range(2) for u in range(2)}
+        zs = {(b, u): keep.tile([P, WIDTH], U8, name="zs%d%d" % (b, u), align_bytes=64) for b in range(2) for u in range(2)}
+        zp = [keep.tile([P, PACK, PAIRS], BF16, name="zp%d" % b) for b in range(2)]
+        hosts, z_tiles = {}, {}
+
+        def pick_host(m, lo, hi):
+            host = ring.tile([P, hi - lo], F32, name="host", tag="host")
+            nc.vector.tensor_copy(host[:], top[m][:].indirect(pos2_sb[:, lo // 16 : hi // 16]))
+            hosts[m, lo] = host
+
+        def pick_difference(m, lo, hi):
+            diff = ring.tile([P, hi - lo], F32, name="diff", tag="diff")
+            nc.vector.tensor_tensor(diff[:], top[m][:].indirect(pos1_sb[:, lo // 16 : hi // 16]), hosts[m, lo][:], ALU.subtract)
+            b, t = divmod(m, PACK)
+            nc.scalar.activation(zp[b][:, t, lo:hi], diff[:], ACT.Copy, scale=gz_sb[:, b, t : t + 1])
+
+        def weave_z(b, u):
+            zg = ring.tile([P, WIDTH, PACK], BF16, name="zg", tag="zg", align_bytes=64)
+            nc.scalar.copy(
+                zg[:].rearrange("p (c i) t -> p c t i", i=4),
+                zp[b][:, :, WIDTH * u : WIDTH * (u + 1)].rearrange("p t (c i) -> p c t i", i=4),
+            )
+            z_tiles[b, u] = zg
+
+        def quantize_z(b, u):
+            nc.vector.quantize_mx(zc[b, u][:].bitcast(FP8X4), zs[b, u][:], z_tiles[b, u][:].rearrange("p n t -> p (n t)"))
+
+        out_view = out.rearrange("(n p) j -> p n j", p=P)
+
+        def last_product(u, v):
+            bank = psum.tile([P, 3, CHUNK], F32, name="bank_y", tag="b")
+            cols = slice(CHUNK * v, CHUNK * (v + 1))
+            for n in range(3):
+                for b in range(2):
+                    nc.tensor.matmul_mx(
+                        bank[:, n, :], lhsT=w3w[:, b, 2 * P * n : 2 * P * (n + 1)].bitcast(FP4X4),
+                        lhsT_scale=w3s[:, b, P * n : P * (n + 1)],
+                        rhs=zc[b, u][:, cols].bitcast(FP8X4), rhs_scale=zs[b, u][:, cols], start=(b == 0), stop=(b == 1),
+                    )
+            res = ring.tile([P, 3, CHUNK], F32, name="res", tag="res")
+            nc.scalar.activation(res[:], bank[:], ACT.Sigmoid)
+            lo = WIDTH * u + CHUNK * v
+            nc.sync.dma_start(out_view[:, :, lo : lo + CHUNK], res[:])
+
+        picks = [(m, 0, PAIRS) for m in range(4)] + [(m, WIDTH * u, WIDTH * (u + 1)) for u in range(2) for m in range(4, 8)]
+        second_product(0, 1)
+        second_product(1, 1)
+        pick_host(*picks[0])
+        for i, pick in enumerate(picks):
+            if i + 2 < 8:
+                second_product(i + 2, 1)
+            if i + 1 < len(picks):
+                pick_host(*picks[i + 1])
+            pick_difference(*pick)
+            if i == 3:
+                weave_z(0, 0)
+                weave_z(0, 1)
+            if i == 5:
+                quantize_z(0, 0)
+            if i == 6:
+                quantize_z(0, 1)
+            if i == 7:
+                weave_z(1, 0)
+            if i == 9:
+                quantize_z(1, 0)
+                last_product(0, 0)
+                last_product(0, 1)
+        weave_z(1, 1)
+        quantize_z(1, 1)
+        last_product(1, 0)
+        last_product(1, 1)

@@ -30,7 +30,7 @@ def tile_list_cuckoo_host_rejection_kernel(
     with ExitStack() as ctx:
         keep = ctx.enter_context(tc.tile_pool(name="keep", bufs=1))
         ring = ctx.enter_context(tc.tile_pool(name="ring", bufs=3))
-        psum = ctx.enter_context(tc.psum_pool(name="psum", bufs=4))
+        psum = ctx.enter_context(tc.psum_pool(name="psum", bufs=1))
 
         offs_sb = keep.tile([P, S // 16], U16, name="offs_sb")
         pos1_sb = keep.tile([P, PAIRS // 16], U16, name="pos1_sb")
@@ -49,12 +49,12 @@ def tile_list_cuckoo_host_rejection_kernel(
         nc.vector.memset(warm[:], 0.0)
         nc.vector.memset(w2s_raw[:].bitcast(I32), 0)
         nc.vector.memset(w3s[:].rearrange("p a n -> p (a n)").bitcast(I32), 0)
-        nc.scalar.activation(warm2[:], warm[:], ACT.Tanh)
 
-        nc.sync.dma_start(offs_sb[:], offs)
         nc.sync.dma_start(tabw[:].bitcast(I32), tab_words[0].bitcast(I32))
+        nc.sync.dma_start(offs_sb[:], offs)
         for q in range(4):
             nc.scalar.dma_start(tabs[32 * q : 32 * q + 4, :].bitcast(I32), tab_scales[0, 4 * q : 4 * q + 4, :].bitcast(I32))
+        nc.scalar.activation(warm2[:], warm[:], ACT.Sigmoid)
         w1_raw = []
         for piece in range(4):
             raw = keep.tile([P, PACK, 256], F32, name="w1_raw%d" % piece)
@@ -80,21 +80,23 @@ def tile_list_cuckoo_host_rejection_kernel(
             )
 
         vw = [keep.tile([P, HALF], U16, name="vw%d" % h, align_bytes=64) for h in range(2)]
-        vs = [keep.tile([P, HALF], U8, name="vs%d" % h, align_bytes=64) for h in range(2)]
+        vs = {}
 
-        def gather_table(h):
-            part = offs_sb[:, 32 * h : 32 * (h + 1)]
-            nc.vector.tensor_copy(vw[h][:], tabw[:].indirect(part))
-            nc.vector.tensor_copy(vs[h][:], tabs[:].indirect(part))
+        def gather_words(h):
+            nc.vector.tensor_copy(vw[h][:], tabw[:].indirect(offs_sb[:, 32 * h : 32 * (h + 1)]))
 
-        w1g = [keep.tile([P, PASS * PACK], BF16, name="w1g%d" % b, align_bytes=64) for b in range(2)]
+        def gather_scales(h, tag):
+            vs[h] = keep.tile([P, HALF], U8, name="vs%d" % h, tag=tag, align_bytes=64)
+            nc.vector.tensor_copy(vs[h][:], tabs[:].indirect(offs_sb[:, 32 * h : 32 * (h + 1)]))
+
+        w1g = [keep.tile([P, PASS * PACK], BF16, name="w1g%d" % b, tag="w1g%d" % b, align_bytes=64) for b in range(2)]
         w1c = [keep.tile([P, PASS], U32, name="w1c%d" % b, align_bytes=64) for b in range(2)]
         w1s = [keep.tile([P, PASS], U8, name="w1s%d" % b, align_bytes=64) for b in range(2)]
 
-        def cast_w1(piece):
+        def cast_w1(copy, piece, lo, hi):
             b, part = divmod(piece, 2)
-            dst = w1g[b][:].rearrange("p (t q j) -> p q t j", t=PACK, j=PACK)[:, 64 * part : 64 * (part + 1), :, :]
-            nc.scalar.copy(dst, w1_raw[piece][:].rearrange("p j (q t) -> p q t j", t=PACK))
+            dst = w1g[b][:].rearrange("p (t q j) -> p q t j", t=PACK, j=PACK)[:, 64 * part + lo : 64 * part + hi, :, :]
+            copy(dst, w1_raw[piece][:].rearrange("p j (q t) -> p q t j", t=PACK)[:, lo:hi, :, :])
 
         def quantize_w1(b):
             nc.vector.quantize_mx(w1c[b][:].bitcast(FP8X4), w1s[b][:], w1g[b][:])
@@ -120,8 +122,8 @@ def tile_list_cuckoo_host_rejection_kernel(
         top = [keep.tile([P, S], F32, name="top%d" % m) for m in range(8)]
         banks, tanh_tiles, x_tiles = {}, {}, {}
 
-        def first_product(b, h, c):
-            bank = psum.tile([P, PACK, CHUNK], F32, name="bank_a", tag="a")
+        def first_product(b, h, c, slot):
+            bank = psum.tile([P, PACK, CHUNK], F32, name="bank_a", tag="bank%d" % slot)
             cols = slice(CHUNK * c, CHUNK * (c + 1))
             for t in range(PACK):
                 rows = slice(P * t, P * (t + 1))
@@ -136,6 +138,20 @@ def tile_list_cuckoo_host_rejection_kernel(
                 tanh_tiles[b, h, c // 2] = ring.tile([P, 2 * CHUNK, PACK], F32, name="th", tag="th")
             dst = tanh_tiles[b, h, c // 2][:, CHUNK * (c % 2) : CHUNK * (c % 2 + 1), :]
             nc.scalar.activation(dst, banks[b, h, c][:].rearrange("p t n -> p n t"), ACT.Tanh)
+
+        def tanh_by_rows(b, h, c):
+            if c % 2 == 0:
+                tanh_tiles[b, h, c // 2] = ring.tile([P, PACK, 2 * CHUNK], F32, name="th", tag="th")
+            dst = tanh_tiles[b, h, c // 2][:, :, CHUNK * (c % 2) : CHUNK * (c % 2 + 1)]
+            nc.scalar.activation(dst, banks[b, h, c][:], ACT.Tanh)
+
+        def gate_x_on_scalar(b, h, u):
+            rows = keep.tile([P, PACK, 2 * CHUNK], BF16, name="x_rows")
+            for t in range(PACK):
+                nc.scalar.activation(rows[:, t, :], tanh_tiles[b, h, u][:, t, :], ACT.Copy, scale=gt_sb[:, b, t : t + 1])
+            xg = ring.tile([P, 2 * CHUNK, PACK], BF16, name="xg", tag="xg", align_bytes=64)
+            nc.scalar.copy(xg[:].rearrange("p (c i) t -> p c t i", i=4), rows[:].rearrange("p t (c i) -> p c t i", i=4))
+            x_tiles[b, h, u] = xg
 
         def keep_a(b, h, c):
             nc.scalar.copy(a_sb[b, h][:, :, CHUNK * c : CHUNK * (c + 1)], banks[b, h, c][:])
@@ -152,8 +168,8 @@ def tile_list_cuckoo_host_rejection_kernel(
                 xc[b, h][:, cols].bitcast(FP8X4), xs[b, h][:, cols], x_tiles[b, h, u][:].rearrange("p n t -> p (n t)")
             )
 
-        def second_product(m, h):
-            bank = psum.tile([P, HALF], F32, name="bank_b", tag="b")
+        def second_product(m, h, slot):
+            bank = psum.tile([P, HALF], F32, name="bank_b", tag="bank%d" % slot)
             rows = slice(P * m, P * (m + 1))
             for g in range(2):
                 nc.tensor.matmul_mx(
@@ -163,107 +179,160 @@ def tile_list_cuckoo_host_rejection_kernel(
             b, t = divmod(m, PACK)
             nc.vector.tensor_tensor(top[m][:, HALF * h : HALF * (h + 1)], bank[:], a_sb[b, h][:, t, :], ALU.max)
 
-        gather_table(0)
-        cast_w1(0)
-        cast_w1(1)
+        gather_words(0)
+        gather_scales(0, "vs0")
+        gather_words(1)
+        cast_w1(nc.scalar.copy, 0, 0, 64)
+        cast_w1(nc.scalar.copy, 1, 0, 64)
         quantize_w1(0)
-        gather_table(1)
+        gather_scales(1, "w1g0")
+        cast_w1(nc.scalar.copy, 2, 0, 64)
+        cast_w1(nc.scalar.copy, 3, 0, 32)
+        cast_w1(nc.vector.tensor_copy, 3, 32, 64)
+        chunks = [(b, h, c) for h in range(2) for b in range(2) for c in range(4)]
+        slots = [0, 1, 2, 3, 4, 5, 6, 7, 2, 3, 4, 5, 6, 7, 2, 3]
         steps = [(b, h, u) for h in range(2) for b in range(2) for u in range(2)]
+        kept = {4: [0, 1, 2, 3], 7: [8, 9]}
         for i, (b, h, u) in enumerate(steps):
-            for c in (2 * u, 2 * u + 1):
-                first_product(b, h, c)
-                tanh_of(b, h, c)
+            for k in kept.get(i, []):
+                keep_a(*chunks[k])
+            for k in (2 * i, 2 * i + 1):
+                first_product(*chunks[k], slots[k])
+                if i == 6:
+                    tanh_by_rows(*chunks[k])
+                else:
+                    tanh_of(*chunks[k])
+            if i != 6:
+                gate_x(b, h, u)
             if i == 0:
-                cast_w1(2)
-                cast_w1(3)
                 quantize_w1(1)
-            gate_x(b, h, u)
-            if i < 6:
-                keep_a(b, h, 2 * u)
-                keep_a(b, h, 2 * u + 1)
-            if i > 0:
+            if i == 5:
+                second_product(0, 0, 0)
+                second_product(1, 0, 1)
+            if i in (1, 2, 3, 5):
                 quantize_x(*steps[i - 1])
+            if i in (3, 5, 7):
+                quantize_x(*steps[i])
             if i == 1:
                 deal_w2_words(0)
                 deal_w2_scales()
-            if i == 2:
                 deal_w2_words(1)
-            if i >= 4:
-                second_product(2 * (i - 4), 0)
-                second_product(2 * (i - 4) + 1, 0)
-        quantize_x(*steps[-1])
-        for c in range(4):
-            keep_a(1, 1, c)
+        gate_x_on_scalar(*steps[6])
+        second_product(2, 0, 0)
+        quantize_x(*steps[6])
+        second_product(3, 0, 1)
+        for k in range(10, 16):
+            keep_a(*chunks[k])
+        for k in range(4, 8):
+            first_product(*chunks[k], slots[k + 8])
+            keep_a(*chunks[k])
 
         WIDTH = 256
         zc = {(b, u): keep.tile([P, WIDTH], U32, name="zc%d%d" % (b, u), align_bytes=64) for b in range(2) for u in range(2)}
         zs = {(b, u): keep.tile([P, WIDTH], U8, name="zs%d%d" % (b, u), align_bytes=64) for b in range(2) for u in range(2)}
         zp = [keep.tile([P, PACK, PAIRS], BF16, name="zp%d" % b) for b in range(2)]
+        last_diff = keep.tile([P, PACK, WIDTH], F32, name="last_diff")
         hosts, z_tiles = {}, {}
 
-        def pick_host(m, lo, hi):
-            host = ring.tile([P, hi - lo], F32, name="host", tag="host")
+        def pick_host(m, lo, hi, after=None):
+            if after is None:
+                host = ring.tile([P, hi - lo], F32, name="host", tag="host")
+            else:
+                host = keep.tile([P, hi - lo], F32, name="host", tag=after, align_bytes=64)
             nc.vector.tensor_copy(host[:], top[m][:].indirect(pos2_sb[:, lo // 16 : hi // 16]))
             hosts[m, lo] = host
 
         def pick_difference(m, lo, hi):
-            diff = ring.tile([P, hi - lo], F32, name="diff", tag="diff")
-            nc.vector.tensor_tensor(diff[:], top[m][:].indirect(pos1_sb[:, lo // 16 : hi // 16]), hosts[m, lo][:], ALU.subtract)
             b, t = divmod(m, PACK)
-            nc.scalar.activation(zp[b][:, t, lo:hi], diff[:], ACT.Copy, scale=gz_sb[:, b, t : t + 1])
+            gain = gz_sb[:, b, t : t + 1]
+            picked = top[m][:].indirect(pos1_sb[:, lo // 16 : hi // 16])
+            if lo == 0:
+                diff = ring.tile([P, hi - lo], F32, name="diff", tag="diff")
+                nc.vector.tensor_tensor(diff[:], picked, hosts[m, lo][:], ALU.subtract)
+                nc.scalar.activation(zp[b][:, t, lo:hi], diff[:], ACT.Copy, scale=gain)
+            else:
+                nc.vector.tensor_tensor(last_diff[:, t, :], picked, hosts[m, lo][:], ALU.subtract)
+                nc.scalar.activation(zp[b][:, t, lo + CHUNK : hi], last_diff[:, t, CHUNK:], ACT.Copy, scale=gain)
 
-        def weave_z(b, u):
-            zg = ring.tile([P, WIDTH, PACK], BF16, name="zg", tag="zg", align_bytes=64)
+        def weave_z(b, lo, hi):
+            zg = keep.tile([P, hi - lo, PACK], BF16, name="zg", tag="zg%d_%d" % (b, lo), align_bytes=64)
             nc.scalar.copy(
-                zg[:].rearrange("p (c i) t -> p c t i", i=4),
-                zp[b][:, :, WIDTH * u : WIDTH * (u + 1)].rearrange("p t (c i) -> p c t i", i=4),
+                zg[:].rearrange("p (c i) t -> p c t i", i=4), zp[b][:, :, lo:hi].rearrange("p t (c i) -> p c t i", i=4)
             )
-            z_tiles[b, u] = zg
+            z_tiles[b, lo] = zg
 
-        def quantize_z(b, u):
-            nc.vector.quantize_mx(zc[b, u][:].bitcast(FP8X4), zs[b, u][:], z_tiles[b, u][:].rearrange("p n t -> p (n t)"))
+        def gate_last():
+            zg = keep.tile([P, CHUNK, PACK], BF16, name="zg_last", align_bytes=64)
+            gain = gz_sb[:, 1, :].unsqueeze(1).to_broadcast([P, CHUNK, PACK])
+            nc.vector.tensor_tensor(zg[:], last_diff[:, :, 0:CHUNK].rearrange("p t n -> p n t"), gain, ALU.mult)
+            z_tiles[1, WIDTH] = zg
+
+        def quantize_z(b, lo, hi):
+            u, start = divmod(lo, WIDTH)
+            cols = slice(start, start + hi - lo)
+            nc.vector.quantize_mx(
+                zc[b, u][:, cols].bitcast(FP8X4), zs[b, u][:, cols], z_tiles[b, lo][:].rearrange("p n t -> p (n t)")
+            )
 
         out_view = out.rearrange("(n p) j -> p n j", p=P)
 
-        def last_product(u, v):
-            bank = psum.tile([P, 3, CHUNK], F32, name="bank_y", tag="b")
+        y_banks = {}
+
+        def last_product(b, u, v):
+            if b == 0:
+                y_banks[u, v] = psum.tile([P, 3, CHUNK], F32, name="bank_y", tag="bank%d" % (2 + 4 * u + v))
             cols = slice(CHUNK * v, CHUNK * (v + 1))
             for n in range(3):
-                for b in range(2):
-                    nc.tensor.matmul_mx(
-                        bank[:, n, :], lhsT=w3w[:, b, 2 * P * n : 2 * P * (n + 1)].bitcast(FP4X4),
-                        lhsT_scale=w3s[:, b, P * n : P * (n + 1)],
-                        rhs=zc[b, u][:, cols].bitcast(FP8X4), rhs_scale=zs[b, u][:, cols], start=(b == 0), stop=(b == 1),
-                    )
+                nc.tensor.matmul_mx(
+                    y_banks[u, v][:, n, :], lhsT=w3w[:, b, 2 * P * n : 2 * P * (n + 1)].bitcast(FP4X4),
+                    lhsT_scale=w3s[:, b, P * n : P * (n + 1)],
+                    rhs=zc[b, u][:, cols].bitcast(FP8X4), rhs_scale=zs[b, u][:, cols],
+                    start=(b == 0 and n == 0), stop=(b == 1 and n == 2),
+                )
+
+        def finish(u, v, queue):
             res = ring.tile([P, 3, CHUNK], F32, name="res", tag="res")
-            nc.scalar.activation(res[:], bank[:], ACT.Sigmoid)
+            nc.scalar.activation(res[:], y_banks[u, v][:], ACT.Sigmoid)
             lo = WIDTH * u + CHUNK * v
-            nc.sync.dma_start(out_view[:, :, lo : lo + CHUNK], res[:])
+            queue.dma_start(out_view[:, :, lo : lo + CHUNK], res[:])
 
         picks = [(m, 0, PAIRS) for m in range(4)] + [(m, WIDTH * u, WIDTH * (u + 1)) for u in range(2) for m in range(4, 8)]
-        second_product(0, 1)
-        second_product(1, 1)
+        behind = {7: "zg0_0", 8: "zg0_256", 11: "zg1_0"}
+        later = [(m, 1) for m in range(4)] + [(m, h) for m in range(4, 8) for h in range(2)]
+        free = [4, 5, 0, 1]
+        second_product(0, 1, 4)
+        second_product(1, 1, 5)
         pick_host(*picks[0])
         for i, pick in enumerate(picks):
-            if i + 2 < 8:
-                second_product(i + 2, 1)
+            for k, (m, h) in enumerate(later):
+                if m == i + 2:
+                    second_product(m, h, free[k % 4])
+            if i == 6:
+                quantize_z(0, 0, WIDTH)
+                last_product(0, 0, 0)
+                last_product(0, 0, 1)
+            if i == 7:
+                quantize_z(0, WIDTH, PAIRS)
+                last_product(0, 1, 0)
+                last_product(0, 1, 1)
+            if i == 10:
+                quantize_z(1, 0, WIDTH)
+                for v in range(2):
+                    last_product(1, 0, v)
+                    finish(0, v, nc.sync)
             if i + 1 < len(picks):
-                pick_host(*picks[i + 1])
+                pick_host(*picks[i + 1], behind.get(i + 1))
             pick_difference(*pick)
             if i == 3:
-                weave_z(0, 0)
-                weave_z(0, 1)
-            if i == 5:
-                quantize_z(0, 0)
-            if i == 6:
-                quantize_z(0, 1)
+                weave_z(0, 0, WIDTH)
+                weave_z(0, WIDTH, PAIRS)
             if i == 7:
-                weave_z(1, 0)
-            if i == 9:
-                quantize_z(1, 0)
-                last_product(0, 0)
-                last_product(0, 1)
-        weave_z(1, 1)
-        quantize_z(1, 1)
-        last_product(1, 0)
-        last_product(1, 1)
+                weave_z(1, 0, WIDTH)
+        gate_last()
+        weave_z(1, WIDTH + CHUNK, PAIRS)
+        quantize_z(1, WIDTH, WIDTH + CHUNK)
+        last_product(1, 1, 0)
+        finish(1, 0, nc.sync)
+        quantize_z(1, WIDTH + CHUNK, PAIRS)
+        last_product(1, 1, 1)
+        finish(1, 1, nc.scalar)

@@ -35,7 +35,7 @@ def tile_list_cuckoo_host_rejection_kernel(
         offs_sb = keep.tile([P, S // 16], U16, name="offs_sb")
         pos1_sb = keep.tile([P, PAIRS // 16], U16, name="pos1_sb")
         pos2_sb = keep.tile([P, PAIRS // 16], U16, name="pos2_sb")
-        tabw = keep.tile([P, T], U16, name="tabw", align_bytes=64)
+        tabw = keep.tile([P, T], U16, name="tabw", tag="tabw", align_bytes=64)
         tabs = keep.tile([P, T], U8, name="tabs", align_bytes=64)
         w2s_raw = keep.tile([P, H], U8, name="w2s_raw", align_bytes=64)
         w3s = keep.tile([P, 2, N], U8, name="w3s", align_bytes=64)
@@ -153,8 +153,8 @@ def tile_list_cuckoo_host_rejection_kernel(
             nc.scalar.copy(xg[:].rearrange("p (c i) t -> p c t i", i=4), rows[:].rearrange("p t (c i) -> p c t i", i=4))
             x_tiles[b, h, u] = xg
 
-        def keep_a(b, h, c):
-            nc.scalar.copy(a_sb[b, h][:, :, CHUNK * c : CHUNK * (c + 1)], banks[b, h, c][:])
+        def keep_a(b, h, c, lo=0, hi=PACK):
+            nc.scalar.copy(a_sb[b, h][:, lo:hi, CHUNK * c : CHUNK * (c + 1)], banks[b, h, c][:, lo:hi, :])
 
         def gate_x(b, h, u):
             xg = ring.tile([P, 2 * CHUNK, PACK], BF16, name="xg", tag="xg", align_bytes=64)
@@ -180,8 +180,8 @@ def tile_list_cuckoo_host_rejection_kernel(
             nc.vector.tensor_tensor(top[m][:, HALF * h : HALF * (h + 1)], bank[:], a_sb[b, h][:, t, :], ALU.max)
 
         gather_words(0)
-        gather_scales(0, "vs0")
         gather_words(1)
+        gather_scales(0, "tabw")
         cast_w1(nc.scalar.copy, 0, 0, 64)
         cast_w1(nc.scalar.copy, 1, 0, 64)
         quantize_w1(0)
@@ -211,7 +211,7 @@ def tile_list_cuckoo_host_rejection_kernel(
                 second_product(1, 0, 1)
             if i in (1, 2, 3, 5):
                 quantize_x(*steps[i - 1])
-            if i in (3, 5, 7):
+            if i in (3, 5):
                 quantize_x(*steps[i])
             if i == 1:
                 deal_w2_words(0)
@@ -219,9 +219,14 @@ def tile_list_cuckoo_host_rejection_kernel(
                 deal_w2_words(1)
         gate_x_on_scalar(*steps[6])
         second_product(2, 0, 0)
+        quantize_x(*steps[7])
         quantize_x(*steps[6])
         second_product(3, 0, 1)
-        for k in range(10, 16):
+        for k in (10, 11):
+            keep_a(*chunks[k])
+        second_product(0, 1, 0)
+        second_product(1, 1, 1)
+        for k in range(12, 16):
             keep_a(*chunks[k])
         for k in range(4, 8):
             first_product(*chunks[k], slots[k + 8])
@@ -299,9 +304,7 @@ def tile_list_cuckoo_host_rejection_kernel(
         picks = [(m, 0, PAIRS) for m in range(4)] + [(m, WIDTH * u, WIDTH * (u + 1)) for u in range(2) for m in range(4, 8)]
         behind = {7: "zg0_0", 8: "zg0_256", 11: "zg1_0"}
         later = [(m, 1) for m in range(4)] + [(m, h) for m in range(4, 8) for h in range(2)]
-        free = [4, 5, 0, 1]
-        second_product(0, 1, 4)
-        second_product(1, 1, 5)
+        free = [0, 1, 4, 5]
         pick_host(*picks[0])
         for i, pick in enumerate(picks):
             for k, (m, h) in enumerate(later):

from contextlib import ExitStack

import concourse.mybir as mybir

K, H, N, T, S, PAIRS = 512, 1024, 384, 2048, 1024, 512
FLOPS = 2 * K * H * S + 2 * H * H * S + 2 * H * N * PAIRS

F32 = mybir.dt.float32
BF16 = mybir.dt.bfloat16
I32 = mybir.dt.int32
U32 = mybir.dt.uint32
U16 = mybir.dt.uint16
U8 = mybir.dt.uint8
FP8X4 = mybir.dt.float8_e4m3fn_x4
FP4X4 = mybir.dt.float4_e2m1fn_x4
ALU = mybir.AluOpType
ACT = mybir.ActivationFunctionType

P = 128
PACK = 4
PASS = P * PACK
HALF = 512
CHUNK = 128


def tile_list_cuckoo_host_rejection_kernel(
    tc, tab_words, tab_scales, offs, pos1, pos2, w1, gt, w2_words, w2_scales, gz, w3_words, w3_scales, out
):
    nc = tc.nc
    with ExitStack() as ctx:
        keep = ctx.enter_context(tc.tile_pool(name="keep", bufs=1))
        ring = ctx.enter_context(tc.tile_pool(name="ring", bufs=3))
        psum = ctx.enter_context(tc.psum_pool(name="psum", bufs=1))

        offs_sb = keep.tile([P, S // 16], U16, name="offs_sb")
        pos1_sb = keep.tile([P, PAIRS // 16], U16, name="pos1_sb")
        pos2_sb = keep.tile([P, PAIRS // 16], U16, name="pos2_sb")
        tabw = keep.tile([P, T], U16, name="tabw", tag="tabw", align_bytes=64)
        tabs = keep.tile([P, T], U8, name="tabs", align_bytes=64)
        w2s_raw = keep.tile([P, H], U8, name="w2s_raw", align_bytes=64)
        w3s = keep.tile([P, 2, N], U8, name="w3s", align_bytes=64)
        w3w = keep.tile([P, 2, 2 * N], U8, name="w3w", align_bytes=64)
        gt_sb = keep.tile([P, 2, PACK], F32, name="gt_sb")
        gz_sb = keep.tile([P, 2, PACK], F32, name="gz_sb")
        warm = keep.tile([P, 8], F32, name="warm")
        warm2 = keep.tile([P, 8], F32, name="warm2")

        nc.vector.memset(tabs[:].bitcast(I32), 0)
        nc.vector.memset(warm[:], 0.0)
        nc.vector.memset(w2s_raw[:].bitcast(I32), 0)
        nc.vector.memset(w3s[:].rearrange("p a n -> p (a n)").bitcast(I32), 0)

        nc.sync.dma_start(tabw[:].bitcast(I32), tab_words[0].bitcast(I32))
        nc.sync.dma_start(offs_sb[:], offs)
        for q in range(4):
            nc.scalar.dma_start(tabs[32 * q : 32 * q + 4, :].bitcast(I32), tab_scales[0, 4 * q : 4 * q + 4, :].bitcast(I32))
        nc.scalar.activation(warm2[:], warm[:], ACT.Sigmoid)
        w1_raw = []
        for piece in range(4):
            raw = keep.tile([P, PACK, 256], F32, name="w1_raw%d" % piece)
            nc.sync.dma_start(raw[:], w1[:, 256 * piece : 256 * (piece + 1)].rearrange("(p j) c -> p j c", j=PACK))
            w1_raw.append(raw)
            if piece == 1:
                nc.sync.dma_start(gt_sb[:], gt.rearrange("(b p t) -> p b t", p=P, t=PACK))
        w2_raw = []
        for g in range(2):
            raw = keep.tile([P, H], U32, name="w2_raw%d" % g)
            nc.sync.dma_start(raw[:].bitcast(I32), w2_words[g].rearrange("p c i -> p (c i)").bitcast(I32))
            w2_raw.append(raw)
        for q in range(4):
            nc.sync.dma_start(w2s_raw[32 * q : 32 * q + 8, :].bitcast(I32), w2_scales[:, 4 * q : 4 * q + 4, :].bitcast(I32))
        nc.sync.dma_start(pos2_sb[:], pos2)
        nc.sync.dma_start(pos1_sb[:], pos1)
        nc.sync.dma_start(gz_sb[:], gz.rearrange("(b p t) -> p b t", p=P, t=PACK))
        nc.sync.dma_start(w3w[:].bitcast(I32), w3_words.rearrange("a p c -> p a c").bitcast(I32))
        for q in range(4):
            nc.sync.dma_start(
                w3s[32 * q : 32 * q + 4, :, :].bitcast(I32),
                w3_scales[:, 4 * q : 4 * q + 4, :].rearrange("a r n -> r a n").bitcast(I32),
            )

        vw = [keep.tile([P, HALF], U16, name="vw%d" % h, align_bytes=64) for h in range(2)]
        vs = {}

        def gather_words(h):
            nc.vector.tensor_copy(vw[h][:], tabw[:].indirect(offs_sb[:, 32 * h : 32 * (h + 1)]))

        def gather_scales(h, tag):
            vs[h] = keep.tile([P, HALF], U8, name="vs%d" % h, tag=tag, align_bytes=64)
            nc.vector.tensor_copy(vs[h][:], tabs[:].indirect(offs_sb[:, 32 * h : 32 * (h + 1)]))

        w1g = [keep.tile([P, PASS * PACK], BF16, name="w1g%d" % b, tag="w1g%d" % b, align_bytes=64) for b in range(2)]
        w1c = [keep.tile([P, PASS], U32, name="w1c%d" % b, align_bytes=64) for b in range(2)]
        w1s = [keep.tile([P, PASS], U8, name="w1s%d" % b, align_bytes=64) for b in range(2)]

        def cast_w1(copy, piece, lo, hi):
            b, part = divmod(piece, 2)
            dst = w1g[b][:].rearrange("p (t q j) -> p q t j", t=PACK, j=PACK)[:, 64 * part + lo : 64 * part + hi, :, :]
            copy(dst, w1_raw[piece][:].rearrange("p j (q t) -> p q t j", t=PACK)[:, lo:hi, :, :])

        def quantize_w1(b):
            nc.vector.quantize_mx(w1c[b][:].bitcast(FP8X4), w1s[b][:], w1g[b][:])

        w2c = [keep.tile([P, H], U32, name="w2c%d" % g, align_bytes=64) for g in range(2)]
        w2s = keep.tile([P, H], U8, name="w2s", align_bytes=64)

        def deal_w2_words(g):
            nc.vector.tensor_copy(
                w2c[g][:].rearrange("p (b t u i) -> p b u t i", b=2, t=PACK, i=4),
                w2_raw[g][:].rearrange("p (b u i t) -> p b u t i", b=2, t=PACK, i=4),
            )

        def deal_w2_scales():
            nc.vector.tensor_copy(
                w2s[:].rearrange("p (b t u i) -> p b u t i", b=2, t=PACK, i=16),
                w2s_raw[:].rearrange("p (b u i t) -> p b u t i", b=2, t=PACK, i=16),
            )

        a_sb = {(b, h): keep.tile([P, PACK, HALF], F32, name="a_sb%d%d" % (b, h)) for b in range(2) for h in range(2)}
        xc = {(b, h): keep.tile([P, HALF], U32, name="xc%d%d" % (b, h), align_bytes=64) for b in range(2) for h in range(2)}
        xs = {(b, h): keep.tile([P, HALF], U8, name="xs%d%d" % (b, h), align_bytes=64) for b in range(2) for h in range(2)}
        top = [keep.tile([P, S], F32, name="top%d" % m) for m in range(8)]
        banks, tanh_tiles, x_tiles = {}, {}, {}

        def first_product(b, h, c, slot):
            bank = psum.tile([P, PACK, CHUNK], F32, name="bank_a", tag="bank%d" % slot)
            cols = slice(CHUNK * c, CHUNK * (c + 1))
            for t in range(PACK):
                rows = slice(P * t, P * (t + 1))
                nc.tensor.matmul_mx(
                    bank[:, t, :], lhsT=w1c[b][:, rows].bitcast(FP8X4), lhsT_scale=w1s[b][:, rows],
                    rhs=vw[h][:, cols].bitcast(FP4X4), rhs_scale=vs[h][:, cols], start=True, stop=True,
                )
            banks[b, h, c] = bank

        def tanh_of(b, h, c):
            if c % 2 == 0:
                tanh_tiles[b, h, c // 2] = ring.tile([P, 2 * CHUNK, PACK], F32, name="th", tag="th")
            dst = tanh_tiles[b, h, c // 2][:, CHUNK * (c % 2) : CHUNK * (c % 2 + 1), :]
            nc.scalar.activation(dst, banks[b, h, c][:].rearrange("p t n -> p n t"), ACT.Tanh)

        def tanh_by_rows(b, h, c):
            if c % 2 == 0:
                tanh_tiles[b, h, c // 2] = ring.tile([P, PACK, 2 * CHUNK], F32, name="th", tag="th")
            dst = tanh_tiles[b, h, c // 2][:, :, CHUNK * (c % 2) : CHUNK * (c % 2 + 1)]
            nc.scalar.activation(dst, banks[b, h, c][:], ACT.Tanh)

        def gate_x_on_scalar(b, h, u):
            rows = keep.tile([P, PACK, 2 * CHUNK], BF16, name="x_rows")
            for t in range(PACK):
                nc.scalar.activation(rows[:, t, :], tanh_tiles[b, h, u][:, t, :], ACT.Copy, scale=gt_sb[:, b, t : t + 1])
            xg = ring.tile([P, 2 * CHUNK, PACK], BF16, name="xg", tag="xg", align_bytes=64)
            nc.scalar.copy(xg[:].rearrange("p (c i) t -> p c t i", i=4), rows[:].rearrange("p t (c i) -> p c t i", i=4))
            x_tiles[b, h, u] = xg

        def keep_a(b, h, c, lo=0, hi=PACK):
            nc.scalar.copy(a_sb[b, h][:, lo:hi, CHUNK * c : CHUNK * (c + 1)], banks[b, h, c][:, lo:hi, :])

        def gate_x(b, h, u):
            xg = ring.tile([P, 2 * CHUNK, PACK], BF16, name="xg", tag="xg", align_bytes=64)
            gain = gt_sb[:, b, :].unsqueeze(1).to_broadcast([P, 2 * CHUNK, PACK])
            nc.vector.tensor_tensor(xg[:], tanh_tiles[b, h, u][:], gain, ALU.mult)
            x_tiles[b, h, u] = xg

        def quantize_x(b, h, u):
            cols = slice(2 * CHUNK * u, 2 * CHUNK * (u + 1))
            nc.vector.quantize_mx(
                xc[b, h][:, cols].bitcast(FP8X4), xs[b, h][:, cols], x_tiles[b, h, u][:].rearrange("p n t -> p (n t)")
            )

        def second_product(m, h, slot):
            bank = psum.tile([P, HALF], F32, name="bank_b", tag="bank%d" % slot)
            rows = slice(P * m, P * (m + 1))
            for g in range(2):
                nc.tensor.matmul_mx(
                    bank[:], lhsT=w2c[g][:, rows].bitcast(FP8X4), lhsT_scale=w2s[4 * g : P, rows],
                    rhs=xc[g, h][:].bitcast(FP8X4), rhs_scale=xs[g, h][:], start=(g == 0), stop=(g == 1),
                )
            b, t = divmod(m, PACK)
            nc.vector.tensor_tensor(top[m][:, HALF * h : HALF * (h + 1)], bank[:], a_sb[b, h][:, t, :], ALU.max)

        gather_words(0)
        gather_words(1)
        gather_scales(0, "tabw")
        cast_w1(nc.scalar.copy, 0, 0, 64)
        cast_w1(nc.scalar.copy, 1, 0, 64)
        quantize_w1(0)
        gather_scales(1, "w1g0")
        cast_w1(nc.scalar.copy, 2, 0, 64)
        cast_w1(nc.scalar.copy, 3, 0, 32)
        cast_w1(nc.vector.tensor_copy, 3, 32, 64)
        chunks = [(b, h, c) for h in range(2) for b in range(2) for c in range(4)]
        slots = [0, 1, 2, 3, 4, 5, 6, 7, 2, 3, 4, 5, 6, 7, 2, 3]
        steps = [(b, h, u) for h in range(2) for b in range(2) for u in range(2)]
        kept = {4: [0, 1, 2, 3], 7: [8, 9]}
        for i, (b, h, u) in enumerate(steps):
            for k in kept.get(i, []):
                keep_a(*chunks[k])
            for k in (2 * i, 2 * i + 1):
                first_product(*chunks[k], slots[k])
                if i == 6:
                    tanh_by_rows(*chunks[k])
                else:
                    tanh_of(*chunks[k])
            if i != 6:
                gate_x(b, h, u)
            if i == 0:
                quantize_w1(1)
            if i == 5:
                second_product(0, 0, 0)
                second_product(1, 0, 1)
            if i in (1, 2, 3, 5):
                quantize_x(*steps[i - 1])
            if i in (3, 5):
                quantize_x(*steps[i])
            if i == 1:
                deal_w2_words(0)
                deal_w2_scales()
                deal_w2_words(1)
        gate_x_on_scalar(*steps[6])
        second_product(2, 0, 0)
        quantize_x(*steps[7])
        quantize_x(*steps[6])
        second_product(3, 0, 1)
        for k in (10, 11):
            keep_a(*chunks[k])
        second_product(0, 1, 0)
        second_product(1, 1, 1)
        for k in range(12, 16):
            keep_a(*chunks[k])
        for k in range(4, 8):
            first_product(*chunks[k], slots[k + 8])
            keep_a(*chunks[k])

        WIDTH = 256
        zc = {(b, u): keep.tile([P, WIDTH], U32, name="zc%d%d" % (b, u), align_bytes=64) for b in range(2) for u in range(2)}
        zs = {(b, u): keep.tile([P, WIDTH], U8, name="zs%d%d" % (b, u), align_bytes=64) for b in range(2) for u in range(2)}
        zp = [keep.tile([P, PACK, PAIRS], BF16, name="zp%d" % b) for b in range(2)]
        last_diff = keep.tile([P, PACK, WIDTH], F32, name="last_diff")
        hosts, z_tiles = {}, {}

        def pick_host(m, lo, hi, after=None):
            if after is None:
                host = ring.tile([P, hi - lo], F32, name="host", tag="host")
            else:
                host = keep.tile([P, hi - lo], F32, name="host", tag=after, align_bytes=64)
            nc.vector.tensor_copy(host[:], top[m][:].indirect(pos2_sb[:, lo // 16 : hi // 16]))
            hosts[m, lo] = host

        def pick_difference(m, lo, hi):
            b, t = divmod(m, PACK)
            gain = gz_sb[:, b, t : t + 1]
            picked = top[m][:].indirect(pos1_sb[:, lo // 16 : hi // 16])
            if lo == 0:
                diff = ring.tile([P, hi - lo], F32, name="diff", tag="diff")
                nc.vector.tensor_tensor(diff[:], picked, hosts[m, lo][:], ALU.subtract)
                nc.scalar.activation(zp[b][:, t, lo:hi], diff[:], ACT.Copy, scale=gain)
            else:
                nc.vector.tensor_tensor(last_diff[:, t, :], picked, hosts[m, lo][:], ALU.subtract)
                nc.scalar.activation(zp[b][:, t, lo + CHUNK : hi], last_diff[:, t, CHUNK:], ACT.Copy, scale=gain)

        def weave_z(b, lo, hi):
            zg = keep.tile([P, hi - lo, PACK], BF16, name="zg", tag="zg%d_%d" % (b, lo), align_bytes=64)
            nc.scalar.copy(
                zg[:].rearrange("p (c i) t -> p c t i", i=4), zp[b][:, :, lo:hi].rearrange("p t (c i) -> p c t i", i=4)
            )
            z_tiles[b, lo] = zg

        def gate_last():
            zg = keep.tile([P, CHUNK, PACK], BF16, name="zg_last", align_bytes=64)
            gain = gz_sb[:, 1, :].unsqueeze(1).to_broadcast([P, CHUNK, PACK])
            nc.vector.tensor_tensor(zg[:], last_diff[:, :, 0:CHUNK].rearrange("p t n -> p n t"), gain, ALU.mult)
            z_tiles[1, WIDTH] = zg

        def quantize_z(b, lo, hi):
            u, start = divmod(lo, WIDTH)
            cols = slice(start, start + hi - lo)
            nc.vector.quantize_mx(
                zc[b, u][:, cols].bitcast(FP8X4), zs[b, u][:, cols], z_tiles[b, lo][:].rearrange("p n t -> p (n t)")
            )

        out_view = out.rearrange("(n p) j -> p n j", p=P)

        y_banks = {}

        def last_product(b, u, v):
            if b == 0:
                y_banks[u, v] = psum.tile([P, 3, CHUNK], F32, name="bank_y", tag="bank%d" % (2 + 4 * u + v))
            cols = slice(CHUNK * v, CHUNK * (v + 1))
            for n in range(3):
                nc.tensor.matmul_mx(
                    y_banks[u, v][:, n, :], lhsT=w3w[:, b, 2 * P * n : 2 * P * (n + 1)].bitcast(FP4X4),
                    lhsT_scale=w3s[:, b, P * n : P * (n + 1)],
                    rhs=zc[b, u][:, cols].bitcast(FP8X4), rhs_scale=zs[b, u][:, cols],
                    start=(b == 0 and n == 0), stop=(b == 1 and n == 2),
                )

        def finish(u, v, queue):
            res = ring.tile([P, 3, CHUNK], F32, name="res", tag="res")
            nc.scalar.activation(res[:], y_banks[u, v][:], ACT.Sigmoid)
            lo = WIDTH * u + CHUNK * v
            queue.dma_start(out_view[:, :, lo : lo + CHUNK], res[:])

        picks = [(m, 0, PAIRS) for m in range(4)] + [(m, WIDTH * u, WIDTH * (u + 1)) for u in range(2) for m in range(4, 8)]
        behind = {7: "zg0_0", 8: "zg0_256", 11: "zg1_0"}
        later = [(m, 1) for m in range(4)] + [(m, h) for m in range(4, 8) for h in range(2)]
        free = [0, 1, 4, 5]
        pick_host(*picks[0])
        for i, pick in enumerate(picks):
            for k, (m, h) in enumerate(later):
                if m == i + 2:
                    second_product(m, h, free[k % 4])
            if i == 6:
                quantize_z(0, 0, WIDTH)
                last_product(0, 0, 0)
                last_product(0, 0, 1)
            if i == 7:
                quantize_z(0, WIDTH, PAIRS)
                last_product(0, 1, 0)
                last_product(0, 1, 1)
            if i == 10:
                quantize_z(1, 0, WIDTH)
                for v in range(2):
                    last_product(1, 0, v)
                    finish(0, v, nc.sync)
            if i + 1 < len(picks):
                pick_host(*picks[i + 1], behind.get(i + 1))
            pick_difference(*pick)
            if i == 3:
                weave_z(0, 0, WIDTH)
                weave_z(0, WIDTH, PAIRS)
            if i == 7:
                weave_z(1, 0, WIDTH)
        gate_last()
        weave_z(1, WIDTH + CHUNK, PAIRS)
        quantize_z(1, WIDTH, WIDTH + CHUNK)
        last_product(1, 1, 0)
        finish(1, 0, nc.sync)
        quantize_z(1, WIDTH + CHUNK, PAIRS)
        last_product(1, 1, 1)
        finish(1, 1, nc.scalar)
